import numpy as np
import ml_dtypes


def mxq(x, axis, fmt="e4m3"):
    dtype, down = {"e4m3": (ml_dtypes.float8_e4m3fn, 7), "e5m2": (ml_dtypes.float8_e5m2, 14)}[fmt]
    v = np.moveaxis(np.asarray(x, np.float32).astype(ml_dtypes.bfloat16).astype(np.float64), axis, -1)
    blocks = v.reshape(v.shape[:-1] + (-1, 32))
    amax = np.abs(blocks).max(-1, keepdims=True)
    byte = np.maximum(np.where(amax > 0, np.frexp(amax)[1] - 1 + 127, 0) - down, 1)
    scale = np.exp2(byte - 127.0)
    codes = (blocks / scale).astype(np.float32).astype(dtype).astype(np.float64)
    return np.moveaxis((codes * scale).reshape(v.shape), -1, axis)


WIDE = False


def mx_kscale(k):
    if not WIDE:
        return np.ones(k)
    levels = np.array([10, -10, 5, -5, 0])
    if k % 512:
        return np.exp2(np.random.permutation(np.resize(levels, k // 32))).repeat(32)
    a = np.empty((k // 512, 16))
    for p in range(k // 512):
        a[p, :8] = np.random.permutation(np.resize(levels, 8))
        for g in range(8):
            far = levels[np.abs(levels - a[p, g]) >= 10]
            a[p, g + 8] = far[np.random.randint(len(far))]
    return np.exp2(a.ravel()).repeat(32)


def f64(x):
    return np.asarray(x).astype(np.float64)


def striped(idx):
    return np.tile(np.asarray(idx).reshape(-1, 16).T, (8, 1)).astype(np.uint16)


def unstriped(offs):
    return offs[:16].T.reshape(-1).astype(np.int64)


def striped8(idx):
    return np.asarray(idx).reshape(8, -1, 16).transpose(0, 2, 1).reshape(128, -1).astype(np.uint16)


def unstriped8(offs):
    return offs.reshape(8, 16, -1).transpose(0, 2, 1).reshape(8, -1).astype(np.int64)


def pick8(x, idx, run):
    r = np.arange(len(x))
    return x[r[:, None], idx[r % (8 * run) // run]]


E2M1 = np.array([0.0, 0.5, 1.0, 1.5, 2.0, 3.0, 4.0, 6.0, -0.0, -0.5, -1.0, -1.5, -2.0, -3.0, -4.0, -6.0])


def pack_weight(w, fmt):
    k, n = w.shape
    w = f64(np.asarray(w, np.float32).astype(ml_dtypes.bfloat16)).reshape(k // 32, 32, n)
    amax = np.abs(w).max(1)
    if fmt == "e4m3":
        byte = np.frexp(amax)[1] - 1 + 127 - 7
    else:
        mant, ex = np.frexp(amax / 6.0)
        byte = np.where(mant > 0.5, ex, ex - 1) + 127
    byte = np.clip(np.where(amax > 0, byte, 1), 1, 254)
    scaled = (w * np.exp2(127.0 - byte)[:, None, :]).reshape(k, n).astype(np.float32)
    by_word = np.ascontiguousarray(scaled.reshape(k // 512, 128, 4, n).transpose(0, 1, 3, 2))
    if fmt == "e4m3":
        words = by_word.astype(ml_dtypes.float8_e4m3fn).view(np.uint8)
    else:
        c = by_word.astype(ml_dtypes.float4_e2m1fn).view(np.uint8) & 0xF
        words = (c[..., 0::2] | (c[..., 1::2] << 4)).reshape(k // 512, 128, 2 * n)
    return np.ascontiguousarray(words), np.ascontiguousarray(byte.astype(np.uint8).reshape(k // 512, 16, n))


def unpack_weight(words, scales, fmt):
    g, _, n = scales.shape
    words = np.ascontiguousarray(words).reshape(g, 128, n, -1)
    if fmt == "e4m3":
        vals = words.view(ml_dtypes.float8_e4m3fn).astype(np.float64)
    else:
        nib = np.empty((g, 128, n, 4), np.uint8)
        nib[..., 0::2] = words & 0xF
        nib[..., 1::2] = words >> 4
        vals = E2M1[nib]
    vals = vals * np.repeat(np.exp2(scales.astype(np.float64) - 127.0), 8, axis=1)[..., None]
    return vals.transpose(0, 1, 3, 2).reshape(g * 512, n)


K, J, R, T, U, F, Z, M, O, C, N = 512, 256, 512, 1024, 1024, 1024, 512, 1024, 128, 512, 256


def setup_inputs():
    n = np.random.standard_normal
    idx = np.stack([np.random.permutation(T)[:J] for _ in range(8)])
    idx2 = np.stack([np.random.permutation(U)[:J] for _ in range(8)])
    idx3 = np.random.permutation(F)[:R]
    idx4 = np.random.permutation(M)[:J]
    idx5 = np.stack([np.random.permutation(C)[:J] for _ in range(8)])
    idx6 = np.stack([np.random.permutation(C)[:O] for _ in range(8)])
    idx7 = np.stack([np.random.permutation(C)[:O] for _ in range(8)])
    fk = mx_kscale(K)
    fr = mx_kscale(R)
    fz = mx_kscale(Z)
    tr = np.ones(F)
    tr[idx3] = fr
    wtp = pack_weight(n((K, F)) * 1 / np.sqrt(K) / fk[:, None] * tr, "e4m3")
    xop = pack_weight(n((Z, M)) / fz[:, None], "e4m3")
    w2p = pack_weight(n((Z, R)) * 1 / np.sqrt(Z) * fz[:, None] * fr, "e2m1")
    wbp = pack_weight(n((R, N)) * 1 / np.sqrt(R) / fr[:, None], "e2m1")
    return {
        "ta": (np.random.randint(-7, 8, (K, T)).astype(np.float64)).astype(np.float32),
        "tb": (np.random.randint(1, 9, (K, U)).astype(np.float64)).astype(np.float32),
        "ga": ((np.random.randint(8, 25, (K, 1)) / 64.0) * fk[:, None]).astype(np.float32),
        "gb": (np.random.uniform(0.1, 0.4, (K, 1))).astype(np.float32),
        "wt_words": wtp[0],
        "wt_scales": wtp[1],
        "xo_words": xop[0],
        "xo_scales": xop[1],
        "w2_words": w2p[0],
        "w2_scales": w2p[1],
        "sa": (np.random.uniform(0.5, 1.6, (R, 1))).astype(np.float32),
        "sb": (np.random.uniform(0.5, 1.6, (R, 1))).astype(np.float32),
        "wb_words": wbp[0],
        "wb_scales": wbp[1],
        "offs": striped8(idx),
        "offs2": striped8(idx2),
        "offs3": striped(idx3),
        "offs4": striped(idx4),
        "offs5": striped8(idx5),
        "offs6": striped8(idx6),
        "offs7": striped8(idx7),
    }


def reference(ta, tb, ga, gb, wt_words, wt_scales, xo_words, xo_scales, w2_words, w2_scales, sa, sb, wb_words, wb_scales, offs, offs2, offs3, offs4, offs5, offs6, offs7):
    idx = unstriped8(offs)
    idx2 = unstriped8(offs2)
    idx3 = unstriped(offs3)
    idx4 = unstriped(offs4)
    idx5 = unstriped8(offs5)
    idx6 = unstriped8(offs6)
    idx7 = unstriped8(offs7)
    wtu = unpack_weight(wt_words, wt_scales, "e4m3")
    xou = unpack_weight(xo_words, xo_scales, "e4m3")
    w2u = unpack_weight(w2_words, w2_scales, "e2m1")
    wbu = unpack_weight(wb_words, wb_scales, "e2m1")
    xc = pick8(f64(ta), idx, 64) * f64(ga) * pick8(f64(tb), idx2, 64) * f64(gb)
    wtidx3g = wtu[:, idx3]
    xcq = mxq(xc, 0, "e4m3")
    xoidx4g = xou[:, idx4]
    a = wtidx3g.T @ xcq + w2u.T @ xoidx4g
    pw = np.zeros((R, C))
    pw[np.arange(R)[:, None], idx5[np.arange(R) % 512 // 64]] = a
    hid = np.abs(pick8(pw, idx6, 64) * f64(sa) - pick8(pw, idx7, 64) * f64(sb))
    hidq = mxq(hid, 0, "e4m3")
    y = wbu.T @ hidq
    return y

@@ -1,0 +1,203 @@
+from contextlib import ExitStack
+
+import concourse.mybir as mybir
+
+FLOPS = 301989888
+
+F32 = mybir.dt.float32
+BF16 = mybir.dt.bfloat16
+I32 = mybir.dt.int32
+U32 = mybir.dt.uint32
+U16 = mybir.dt.uint16
+U8 = mybir.dt.uint8
+FP8X4 = mybir.dt.float8_e4m3fn_x4
+FP4X4 = mybir.dt.float4_e2m1fn_x4
+ACT = mybir.ActivationFunctionType
+ALU = mybir.AluOpType
+
+P = 128
+PACK = 4
+QUAD = 32
+J, R, T, M, O, C, N = 256, 512, 1024, 1024, 128, 512, 256
+WT_ROW = 4
+
+
+def tile_picked_codegain_store_bank_boardpair_one_plain_kernel(
+    tc, ta, tb, ga, gb, wt_words, wt_scales, xo_words, xo_scales, w2_words, w2_scales, sa, sb,
+    wb_words, wb_scales, offs, offs2, offs3, offs4, offs5, offs6, offs7, out,
+):
+    nc = tc.nc
+    with ExitStack() as ctx:
+        lists = ctx.enter_context(tc.tile_pool(name="lists", bufs=1))
+        keep = ctx.enter_context(tc.tile_pool(name="keep", bufs=1))
+        psum = ctx.enter_context(tc.psum_pool(name="psum", bufs=1))
+
+        def sbuf(name, shape, dtype):
+            return keep.tile(shape, dtype, name=name, align_bytes=64)
+
+        def load_list(name, src):
+            tile = lists.tile(list(src.shape), U16, name=name)
+            nc.sync.dma_start(tile[:], src)
+            return tile
+
+        def load_column(name, src, queue):
+            tile = sbuf(name, [P, PACK], F32)
+            queue.dma_start(out=tile[:], in_=src.rearrange("(p t) o -> p (t o)", t=PACK))
+            return tile
+
+        def load_rows(name, src, t):
+            tile = sbuf(name, [P, T], F32)
+            nc.sync.dma_start(out=tile[:], in_=src.rearrange("(p t) c -> p t c", t=PACK)[:, t, :])
+            return tile
+
+        def load_scale_rows(stage, first, src):
+            nc.sync.dma_start(
+                out=stage[first:first + 4, :, :].bitcast(I32),
+                in_=src[0].rearrange("(q i) n -> i q n", i=4).bitcast(I32),
+            )
+
+        def spread_scale_rows(plane, stage, first, rows):
+            for q in range(4):
+                nc.vector.tensor_copy(
+                    out=plane[QUAD * q:QUAD * q + rows, :].bitcast(I32),
+                    in_=stage[first:first + rows, q, :].bitcast(I32),
+                )
+
+        wt_stage = sbuf("wt_stage", [QUAD, 4, T], U8)
+        nc.vector.memset(wt_stage[:].rearrange("p q n -> p (q n)").bitcast(I32), 0)
+        w2_stage = sbuf("w2_stage", [P, 4, R], U8)
+        nc.vector.memset(w2_stage[64:96].rearrange("p q n -> p (q n)").bitcast(I32), 0)
+        xo_plane = sbuf("xo_plane", [P, M], U8)
+        nc.vector.memset(xo_plane[:].bitcast(I32), 0)
+        wb_plane = sbuf("wb_plane", [P, N], U8)
+        nc.vector.memset(wb_plane[:].bitcast(I32), 0)
+        board = [sbuf("board%d" % t, [P, C], F32) for t in range(PACK)]
+        for t in range(PACK):
+            nc.vector.memset(board[t][:], 0.0)
+
+        ga_sb = load_column("ga_sb", ga, nc.scalar)
+        gb_sb = load_column("gb_sb", gb, nc.scalar)
+        wt_sb = sbuf("wt_sb", [P, T], U32)
+        nc.sync.dma_start(out=wt_sb[:].bitcast(I32), in_=wt_words[0].rearrange("p n t -> p (n t)").bitcast(I32))
+        l3 = load_list("l3", offs3)
+        load_scale_rows(wt_stage, WT_ROW, wt_scales)
+        l1 = load_list("l1", offs)
+        ta_sb, tb_sb = [], []
+        ta_sb.append(load_rows("ta0", ta, 0))
+        l2 = load_list("l2", offs2)
+        tb_sb.append(load_rows("tb0", tb, 0))
+        xo_stage = sbuf("xo_stage", [4, 4, M], U8)
+        load_scale_rows(xo_stage, 0, xo_scales)
+        l4 = load_list("l4", offs4)
+        ta_sb.append(load_rows("ta1", ta, 1))
+        tb_sb.append(load_rows("tb1", tb, 1))
+        load_scale_rows(w2_stage, 64, w2_scales)
+        w2_sb = sbuf("w2_sb", [P, 2 * R], U8)
+        nc.sync.dma_start(out=w2_sb[:].bitcast(I32), in_=w2_words[0].bitcast(I32))
+        ta_sb.append(load_rows("ta2", ta, 2))
+        tb_sb.append(load_rows("tb2", tb, 2))
+        l5 = load_list("l5", offs5)
+        l6 = load_list("l6", offs6)
+        l7 = load_list("l7", offs7)
+        ta_sb.append(load_rows("ta3", ta, 3))
+        tb_sb.append(load_rows("tb3", tb, 3))
+        xo_sb = sbuf("xo_sb", [P, M], U32)
+        nc.sync.dma_start(out=xo_sb[:].bitcast(I32), in_=xo_words[0].rearrange("p n t -> p (n t)").bitcast(I32))
+        wb_sb = sbuf("wb_sb", [P, 2 * N], U8)
+        nc.sync.dma_start(out=wb_sb[:].bitcast(I32), in_=wb_words[0].bitcast(I32))
+        sa_sb = load_column("sa_sb", sa, nc.gpsimd)
+        sb_sb = load_column("sb_sb", sb, nc.gpsimd)
+        for q in range(4):
+            nc.gpsimd.dma_start(
+                out=wb_plane[QUAD * q:QUAD * q + 4, :].bitcast(I32),
+                in_=wb_scales[0, 4 * q:4 * q + 4, :].bitcast(I32),
+            )
+
+        wt_codes = sbuf("wt_codes", [P, PACK, P], U32)
+        nc.vector.tensor_copy(out=wt_codes[:].rearrange("p t m -> p m t"), in_=wt_sb[:].indirect(l3[:]))
+        wt_plane = sbuf("wt_plane", [P, T], U8)
+        spread_scale_rows(wt_plane, wt_stage, 0, QUAD)
+        wt_bytes = sbuf("wt_bytes", [P, PACK, P], U8)
+        nc.vector.tensor_copy(out=wt_bytes[:].rearrange("p t m -> p m t"), in_=wt_plane[:].indirect(l3[:]))
+
+        spread_scale_rows(xo_plane, xo_stage, 0, 4)
+        xo_bytes = sbuf("xo_bytes", [P, J], U8)
+        nc.vector.tensor_copy(out=xo_bytes[:], in_=xo_plane[:].indirect(l4[:]))
+
+        w2_plane = sbuf("w2_plane", [P, R], U8)
+        spread_scale_rows(w2_plane, w2_stage, 64, QUAD)
+        w2_bytes = sbuf("w2_bytes", [P, PACK, P], U8)
+        nc.vector.tensor_copy(out=w2_bytes[:], in_=w2_plane[:].rearrange("p (m t) -> p t m", t=PACK))
+        w2_codes = sbuf("w2_codes", [P, 2 * R], U8)
+        nc.scalar.copy(
+            out=w2_codes[:].bitcast(U16).rearrange("p (t m) -> p t m", t=PACK),
+            in_=w2_sb[:].bitcast(U16).rearrange("p (m t) -> p t m", t=PACK),
+        )
+
+        xa = sbuf("xa", [P, PACK, J], F32)
+        xb = sbuf("xb", [P, PACK, J], F32)
+        xc = sbuf("xc", [P, PACK, J], F32)
+        for t in range(PACK):
+            nc.scalar.activation(out=xa[:, t, :], in_=ta_sb[t][:].indirect(l1[:]), func=ACT.Copy, scale=ga_sb[:, t:t + 1])
+            nc.scalar.activation(out=xb[:, t, :], in_=tb_sb[t][:].indirect(l2[:]), func=ACT.Copy, scale=gb_sb[:, t:t + 1])
+            nc.vector.tensor_tensor(out=xc[:, t, :], in0=xa[:, t, :], in1=xb[:, t, :], op=ALU.mult)
+        xc_bf = sbuf("xc_bf", [P, J, PACK], BF16)
+        nc.vector.tensor_copy(
+            out=xc_bf[:].rearrange("p (c i) t -> p c t i", i=4),
+            in_=xc[:].rearrange("p t (c i) -> p c t i", i=4),
+        )
+        xc_codes = sbuf("xc_codes", [P, J], U32)
+        xc_bytes = sbuf("xc_bytes", [P, J], U8)
+        nc.vector.quantize_mx(out=xc_codes[:].bitcast(FP8X4), scales=xc_bytes[:], in_=xc_bf[:].rearrange("p j t -> p (j t)"))
+
+        acc = [psum.tile([P, J], F32, name="acc%d" % t) for t in range(PACK)]
+        for t in range(PACK):
+            nc.tensor.matmul_mx(
+                out=acc[t][:], lhsT=wt_codes[:, t, :].bitcast(FP8X4), lhsT_scale=wt_bytes[WT_ROW:P, t, :],
+                rhs=xc_codes[:].bitcast(FP8X4), rhs_scale=xc_bytes[:], start=True, stop=False,
+            )
+        xo_codes = sbuf("xo_codes", [P, J], U32)
+        nc.vector.tensor_copy(out=xo_codes[:], in_=xo_sb[:].indirect(l4[:]))
+
+        first = sbuf("first", [P, PACK, O], F32)
+        second = sbuf("second", [P, PACK, O], F32)
+        for t in range(PACK):
+            nc.tensor.matmul_mx(
+                out=acc[t][:], lhsT=w2_codes[:, 2 * P * t:2 * P * (t + 1)].bitcast(FP4X4), lhsT_scale=w2_bytes[:, t, :],
+                rhs=xo_codes[:].bitcast(FP8X4), rhs_scale=xo_bytes[:], start=False, stop=True,
+            )
+        hidden = [sbuf("hidden%d" % t, [P, J], F32) for t in range(PACK)]
+        for t in range(PACK):
+            nc.scalar.copy(out=hidden[t][:], in_=acc[t][:])
+        for t in range(PACK):
+            nc.vector.tensor_copy(out=board[t][:].indirect(l5[:]), in_=hidden[t][:])
+            nc.scalar.activation(out=first[:, t, :], in_=board[t][:].indirect(l6[:]), func=ACT.Copy, scale=sa_sb[:, t:t + 1])
+            nc.scalar.activation(out=second[:, t, :], in_=board[t][:].indirect(l7[:]), func=ACT.Copy, scale=sb_sb[:, t:t + 1])
+
+        diff = sbuf("diff", [P, PACK, O], F32)
+        nc.vector.tensor_tensor(out=diff[:, 0:3, :], in0=first[:, 0:3, :], in1=second[:, 0:3, :], op=ALU.subtract)
+        nc.vector.tensor_tensor(out=diff[:, 3, :], in0=first[:, 3, :], in1=second[:, 3, :], op=ALU.subtract)
+        hid_bf = sbuf("hid_bf", [P, O, PACK], BF16)
+        turned = diff[:].rearrange("p t o -> p o t")
+        half = O // 2
+        nc.scalar.activation(out=hid_bf[:, 0:half, :], in_=turned[:, 0:half, :], func=ACT.Abs)
+        nc.vector.scalar_tensor_tensor(
+            out=hid_bf[:, half:O, :], in0=turned[:, half:O, :], scalar=-1.0, in1=turned[:, half:O, :],
+            op0=ALU.mult, op1=ALU.max,
+        )
+        hid_codes = sbuf("hid_codes", [P, O], U32)
+        hid_bytes = sbuf("hid_bytes", [P, O], U8)
+        nc.vector.quantize_mx(out=hid_codes[:].bitcast(FP8X4), scales=hid_bytes[:], in_=hid_bf[:].rearrange("p o t -> p (o t)"))
+
+        result = sbuf("result", [P, 2, O], F32)
+        for s in range(2):
+            final = psum.tile([P, O], F32, name="final%d" % s)
+            nc.tensor.matmul_mx(
+                out=final[:], lhsT=wb_sb[:, 2 * P * s:2 * P * (s + 1)].bitcast(FP4X4), lhsT_scale=wb_plane[:, P * s:P * (s + 1)],
+                rhs=hid_codes[:].bitcast(FP8X4), rhs_scale=hid_bytes[:], start=True, stop=True,
+            )
+            if s == 0:
+                nc.scalar.copy(out=result[:, s, :], in_=final[:])
+            else:
+                nc.vector.tensor_copy(out=result[:, s, :], in_=final[:])
+        nc.sync.dma_start(out=out.rearrange("(s p) o -> p s o", p=P), in_=result[:])

@@ -51,7 +51,7 @@ def tile_picked_codegain_store_bank_boardpair_one_plain_kernel(
             return tile
 
         def load_scale_rows(stage, first, src):
-            nc.sync.dma_start(
+            nc.gpsimd.dma_start(
                 out=stage[first:first + 4, :, :].bitcast(I32),
                 in_=src[0].rearrange("(q i) n -> i q n", i=4).bitcast(I32),
             )
@@ -75,43 +75,43 @@ def tile_picked_codegain_store_bank_boardpair_one_plain_kernel(
         for t in range(PACK):
             nc.vector.memset(board[t][:], 0.0)
 
-        ga_sb = load_column("ga_sb", ga, nc.scalar)
-        gb_sb = load_column("gb_sb", gb, nc.scalar)
-        wt_sb = sbuf("wt_sb", [P, T], U32)
-        nc.sync.dma_start(out=wt_sb[:].bitcast(I32), in_=wt_words[0].rearrange("p n t -> p (n t)").bitcast(I32))
-        l3 = load_list("l3", offs3)
-        load_scale_rows(wt_stage, WT_ROW, wt_scales)
-        l1 = load_list("l1", offs)
-        ta_sb, tb_sb = [], []
-        ta_sb.append(load_rows("ta0", ta, 0))
-        l2 = load_list("l2", offs2)
-        tb_sb.append(load_rows("tb0", tb, 0))
         xo_stage = sbuf("xo_stage", [4, 4, M], U8)
         load_scale_rows(xo_stage, 0, xo_scales)
-        l4 = load_list("l4", offs4)
-        ta_sb.append(load_rows("ta1", ta, 1))
-        tb_sb.append(load_rows("tb1", tb, 1))
+        load_scale_rows(wt_stage, WT_ROW, wt_scales)
         load_scale_rows(w2_stage, 64, w2_scales)
-        w2_sb = sbuf("w2_sb", [P, 2 * R], U8)
-        nc.sync.dma_start(out=w2_sb[:].bitcast(I32), in_=w2_words[0].bitcast(I32))
-        ta_sb.append(load_rows("ta2", ta, 2))
-        tb_sb.append(load_rows("tb2", tb, 2))
-        l5 = load_list("l5", offs5)
-        l6 = load_list("l6", offs6)
-        l7 = load_list("l7", offs7)
-        ta_sb.append(load_rows("ta3", ta, 3))
-        tb_sb.append(load_rows("tb3", tb, 3))
-        xo_sb = sbuf("xo_sb", [P, M], U32)
-        nc.sync.dma_start(out=xo_sb[:].bitcast(I32), in_=xo_words[0].rearrange("p n t -> p (n t)").bitcast(I32))
-        wb_sb = sbuf("wb_sb", [P, 2 * N], U8)
-        nc.sync.dma_start(out=wb_sb[:].bitcast(I32), in_=wb_words[0].bitcast(I32))
-        sa_sb = load_column("sa_sb", sa, nc.gpsimd)
-        sb_sb = load_column("sb_sb", sb, nc.gpsimd)
         for q in range(4):
             nc.gpsimd.dma_start(
                 out=wb_plane[QUAD * q:QUAD * q + 4, :].bitcast(I32),
                 in_=wb_scales[0, 4 * q:4 * q + 4, :].bitcast(I32),
             )
+        ga_sb = load_column("ga_sb", ga, nc.scalar)
+        gb_sb = load_column("gb_sb", gb, nc.scalar)
+        wt_sb = sbuf("wt_sb", [P, T], U32)
+        nc.sync.dma_start(out=wt_sb[:].bitcast(I32), in_=wt_words[0].rearrange("p n t -> p (n t)").bitcast(I32))
+        l3 = load_list("l3", offs3)
+        l1 = load_list("l1", offs)
+        ta_sb, tb_sb = [], []
+        ta_sb.append(load_rows("ta0", ta, 0))
+        l2 = load_list("l2", offs2)
+        tb_sb.append(load_rows("tb0", tb, 0))
+        l4 = load_list("l4", offs4)
+        ta_sb.append(load_rows("ta1", ta, 1))
+        l6 = load_list("l6", offs6)
+        tb_sb.append(load_rows("tb1", tb, 1))
+        l7 = load_list("l7", offs7)
+        ta_sb.append(load_rows("ta2", ta, 2))
+        sa_sb = load_column("sa_sb", sa, nc.sync)
+        tb_sb.append(load_rows("tb2", tb, 2))
+        sb_sb = load_column("sb_sb", sb, nc.sync)
+        ta_sb.append(load_rows("ta3", ta, 3))
+        l5 = load_list("l5", offs5)
+        tb_sb.append(load_rows("tb3", tb, 3))
+        xo_sb = sbuf("xo_sb", [P, M], U32)
+        nc.sync.dma_start(out=xo_sb[:].bitcast(I32), in_=xo_words[0].rearrange("p n t -> p (n t)").bitcast(I32))
+        w2_sb = sbuf("w2_sb", [P, 2 * R], U8)
+        nc.sync.dma_start(out=w2_sb[:].bitcast(I32), in_=w2_words[0].bitcast(I32))
+        wb_sb = sbuf("wb_sb", [P, 2 * N], U8)
+        nc.sync.dma_start(out=wb_sb[:].bitcast(I32), in_=wb_words[0].bitcast(I32))
 
         wt_codes = sbuf("wt_codes", [P, PACK, P], U32)
         nc.vector.tensor_copy(out=wt_codes[:].rearrange("p t m -> p m t"), in_=wt_sb[:].indirect(l3[:]))
@@ -128,44 +128,52 @@ def tile_picked_codegain_store_bank_boardpair_one_plain_kernel(
         spread_scale_rows(w2_plane, w2_stage, 64, QUAD)
         w2_bytes = sbuf("w2_bytes", [P, PACK, P], U8)
         nc.vector.tensor_copy(out=w2_bytes[:], in_=w2_plane[:].rearrange("p (m t) -> p t m", t=PACK))
+
+        xa = sbuf("xa", [P, PACK, J], F32)
+        xb = sbuf("xb", [P, PACK, J], F32)
+        xc_bf = sbuf("xc_bf", [P, J, PACK], BF16)
+        for t in range(PACK):
+            nc.scalar.activation(out=xa[:, t, :], in_=ta_sb[t][:].indirect(l1[:]), func=ACT.Copy, scale=ga_sb[:, t:t + 1])
+            nc.scalar.activation(out=xb[:, t, :], in_=tb_sb[t][:].indirect(l2[:]), func=ACT.Copy, scale=gb_sb[:, t:t + 1])
+            if t % 2 == 1:
+                pair = slice(t - 1, t + 1)
+                nc.vector.tensor_tensor(
+                    out=xc_bf[:, :, pair], in0=xa[:, pair, :].rearrange("p t j -> p j t"),
+                    in1=xb[:, pair, :].rearrange("p t j -> p j t"), op=ALU.mult,
+                )
+        xo_codes = sbuf("xo_codes", [P, J], U32)
+        nc.vector.tensor_copy(out=xo_codes[:], in_=xo_sb[:].indirect(l4[:]))
         w2_codes = sbuf("w2_codes", [P, 2 * R], U8)
         nc.scalar.copy(
             out=w2_codes[:].bitcast(U16).rearrange("p (t m) -> p t m", t=PACK),
             in_=w2_sb[:].bitcast(U16).rearrange("p (m t) -> p t m", t=PACK),
-        )
-
-        xa = sbuf("xa", [P, PACK, J], F32)
-        xb = sbuf("xb", [P, PACK, J], F32)
-        xc = sbuf("xc", [P, PACK, J], F32)
-        for t in range(PACK):
-            nc.scalar.activation(out=xa[:, t, :], in_=ta_sb[t][:].indirect(l1[:]), func=ACT.Copy, scale=ga_sb[:, t:t + 1])
-            nc.scalar.activation(out=xb[:, t, :], in_=tb_sb[t][:].indirect(l2[:]), func=ACT.Copy, scale=gb_sb[:, t:t + 1])
-            nc.vector.tensor_tensor(out=xc[:, t, :], in0=xa[:, t, :], in1=xb[:, t, :], op=ALU.mult)
-        xc_bf = sbuf("xc_bf", [P, J, PACK], BF16)
-        nc.vector.tensor_copy(
-            out=xc_bf[:].rearrange("p (c i) t -> p c t i", i=4),
-            in_=xc[:].rearrange("p t (c i) -> p c t i", i=4),
         )
         xc_codes = sbuf("xc_codes", [P, J], U32)
         xc_bytes = sbuf("xc_bytes", [P, J], U8)
         nc.vector.quantize_mx(out=xc_codes[:].bitcast(FP8X4), scales=xc_bytes[:], in_=xc_bf[:].rearrange("p j t -> p (j t)"))
 
         acc = [psum.tile([P, J], F32, name="acc%d" % t) for t in range(PACK)]
-        for t in range(PACK):
+
+        def store_pass(t, opens):
             nc.tensor.matmul_mx(
                 out=acc[t][:], lhsT=wt_codes[:, t, :].bitcast(FP8X4), lhsT_scale=wt_bytes[WT_ROW:P, t, :],
-                rhs=xc_codes[:].bitcast(FP8X4), rhs_scale=xc_bytes[:], start=True, stop=False,
+                rhs=xc_codes[:].bitcast(FP8X4), rhs_scale=xc_bytes[:], start=opens, stop=not opens,
             )
-        xo_codes = sbuf("xo_codes", [P, J], U32)
-        nc.vector.tensor_copy(out=xo_codes[:], in_=xo_sb[:].indirect(l4[:]))
+
+        def notes_pass(t, opens):
+            nc.tensor.matmul_mx(
+                out=acc[t][:], lhsT=w2_codes[:, 2 * P * t:2 * P * (t + 1)].bitcast(FP4X4), lhsT_scale=w2_bytes[:, t, :],
+                rhs=xo_codes[:].bitcast(FP8X4), rhs_scale=xo_bytes[:], start=opens, stop=not opens,
+            )
+
+        store_pass(0, True)
+        notes_pass(0, False)
+        for t in range(1, PACK):
+            notes_pass(t, True)
+            store_pass(t, False)
 
         first = sbuf("first", [P, PACK, O], F32)
         second = sbuf("second", [P, PACK, O], F32)
-        for t in range(PACK):
-            nc.tensor.matmul_mx(
-                out=acc[t][:], lhsT=w2_codes[:, 2 * P * t:2 * P * (t + 1)].bitcast(FP4X4), lhsT_scale=w2_bytes[:, t, :],
-                rhs=xo_codes[:].bitcast(FP8X4), rhs_scale=xo_bytes[:], start=False, stop=True,
-            )
         hidden = [sbuf("hidden%d" % t, [P, J], F32) for t in range(PACK)]
         for t in range(PACK):
             nc.scalar.copy(out=hidden[t][:], in_=acc[t][:])
@@ -189,15 +197,12 @@ def tile_picked_codegain_store_bank_boardpair_one_plain_kernel(
         hid_bytes = sbuf("hid_bytes", [P, O], U8)
         nc.vector.quantize_mx(out=hid_codes[:].bitcast(FP8X4), scales=hid_bytes[:], in_=hid_bf[:].rearrange("p o t -> p (o t)"))
 
-        result = sbuf("result", [P, 2, O], F32)
-        for s in range(2):
+        for s, (copy, queue) in enumerate(((nc.scalar.copy, nc.scalar), (nc.vector.tensor_copy, nc.sync))):
             final = psum.tile([P, O], F32, name="final%d" % s)
             nc.tensor.matmul_mx(
                 out=final[:], lhsT=wb_sb[:, 2 * P * s:2 * P * (s + 1)].bitcast(FP4X4), lhsT_scale=wb_plane[:, P * s:P * (s + 1)],
                 rhs=hid_codes[:].bitcast(FP8X4), rhs_scale=hid_bytes[:], start=True, stop=True,
             )
-            if s == 0:
-                nc.scalar.copy(out=result[:, s, :], in_=final[:])
-            else:
-                nc.vector.tensor_copy(out=result[:, s, :], in_=final[:])
-        nc.sync.dma_start(out=out.rearrange("(s p) o -> p s o", p=P), in_=result[:])
+            result = sbuf("result%d" % s, [P, O], F32)
+            copy(out=result[:], in_=final[:])
+            queue.dma_start(out=out[P * s:P * (s + 1), :], in_=result[:])

@@ -32,8 +32,8 @@ def tile_picked_codegain_store_bank_boardpair_one_plain_kernel(
         keep = ctx.enter_context(tc.tile_pool(name="keep", bufs=1))
         psum = ctx.enter_context(tc.psum_pool(name="psum", bufs=1))
 
-        def sbuf(name, shape, dtype):
-            return keep.tile(shape, dtype, name=name, align_bytes=64)
+        def sbuf(name, shape, dtype, tag=None):
+            return keep.tile(shape, dtype, name=name, tag=tag or name, align_bytes=64)
 
         def load_list(name, src):
             tile = lists.tile(list(src.shape), U16, name=name)
@@ -56,6 +56,12 @@ def tile_picked_codegain_store_bank_boardpair_one_plain_kernel(
                 in_=src[0].rearrange("(q i) n -> i q n", i=4).bitcast(I32),
             )
 
+        def load_plane_rows(plane, src, q):
+            nc.sync.dma_start(
+                out=plane[QUAD * q:QUAD * q + 4, :].bitcast(I32),
+                in_=src[0, 4 * q:4 * q + 4, :].bitcast(I32),
+            )
+
         def spread_scale_rows(plane, stage, first, rows):
             for q in range(4):
                 nc.vector.tensor_copy(
@@ -65,25 +71,19 @@ def tile_picked_codegain_store_bank_boardpair_one_plain_kernel(
 
         wt_stage = sbuf("wt_stage", [QUAD, 4, T], U8)
         nc.vector.memset(wt_stage[:].rearrange("p q n -> p (q n)").bitcast(I32), 0)
-        w2_stage = sbuf("w2_stage", [P, 4, R], U8)
-        nc.vector.memset(w2_stage[64:96].rearrange("p q n -> p (q n)").bitcast(I32), 0)
+        w2_plane = sbuf("w2_plane", [P, R], U8)
+        nc.vector.memset(w2_plane[:].bitcast(I32), 0)
         xo_plane = sbuf("xo_plane", [P, M], U8)
         nc.vector.memset(xo_plane[:].bitcast(I32), 0)
         wb_plane = sbuf("wb_plane", [P, N], U8)
         nc.vector.memset(wb_plane[:].bitcast(I32), 0)
-        board = [sbuf("board%d" % t, [P, C], F32) for t in range(PACK)]
-        for t in range(PACK):
-            nc.vector.memset(board[t][:], 0.0)
 
         xo_stage = sbuf("xo_stage", [4, 4, M], U8)
         load_scale_rows(xo_stage, 0, xo_scales)
         load_scale_rows(wt_stage, WT_ROW, wt_scales)
-        load_scale_rows(w2_stage, 64, w2_scales)
-        for q in range(4):
-            nc.gpsimd.dma_start(
-                out=wb_plane[QUAD * q:QUAD * q + 4, :].bitcast(I32),
-                in_=wb_scales[0, 4 * q:4 * q + 4, :].bitcast(I32),
-            )
+        board = [sbuf("board%d" % t, [P, C], F32) for t in range(PACK)]
+        for t in range(PACK):
+            nc.gpsimd.memset(board[t][:], 0.0)
         ga_sb = load_column("ga_sb", ga, nc.scalar)
         gb_sb = load_column("gb_sb", gb, nc.scalar)
         wt_sb = sbuf("wt_sb", [P, T], U32)
@@ -96,22 +96,28 @@ def tile_picked_codegain_store_bank_boardpair_one_plain_kernel(
         tb_sb.append(load_rows("tb0", tb, 0))
         l4 = load_list("l4", offs4)
         ta_sb.append(load_rows("ta1", ta, 1))
-        l6 = load_list("l6", offs6)
+        load_plane_rows(w2_plane, w2_scales, 0)
         tb_sb.append(load_rows("tb1", tb, 1))
-        l7 = load_list("l7", offs7)
+        load_plane_rows(w2_plane, w2_scales, 1)
         ta_sb.append(load_rows("ta2", ta, 2))
-        sa_sb = load_column("sa_sb", sa, nc.sync)
+        load_plane_rows(w2_plane, w2_scales, 2)
         tb_sb.append(load_rows("tb2", tb, 2))
-        sb_sb = load_column("sb_sb", sb, nc.sync)
+        load_plane_rows(w2_plane, w2_scales, 3)
         ta_sb.append(load_rows("ta3", ta, 3))
-        l5 = load_list("l5", offs5)
+        sa_sb = load_column("sa_sb", sa, nc.sync)
         tb_sb.append(load_rows("tb3", tb, 3))
-        xo_sb = sbuf("xo_sb", [P, M], U32)
-        nc.sync.dma_start(out=xo_sb[:].bitcast(I32), in_=xo_words[0].rearrange("p n t -> p (n t)").bitcast(I32))
+        sb_sb = load_column("sb_sb", sb, nc.sync)
         w2_sb = sbuf("w2_sb", [P, 2 * R], U8)
         nc.sync.dma_start(out=w2_sb[:].bitcast(I32), in_=w2_words[0].bitcast(I32))
+        xo_sb = sbuf("xo_sb", [P, M], U32)
+        nc.sync.dma_start(out=xo_sb[:].bitcast(I32), in_=xo_words[0].rearrange("p n t -> p (n t)").bitcast(I32))
+        l5 = load_list("l5", offs5)
+        l6 = load_list("l6", offs6)
+        l7 = load_list("l7", offs7)
         wb_sb = sbuf("wb_sb", [P, 2 * N], U8)
         nc.sync.dma_start(out=wb_sb[:].bitcast(I32), in_=wb_words[0].bitcast(I32))
+        for q in range(4):
+            load_plane_rows(wb_plane, wb_scales, q)
 
         wt_codes = sbuf("wt_codes", [P, PACK, P], U32)
         nc.vector.tensor_copy(out=wt_codes[:].rearrange("p t m -> p m t"), in_=wt_sb[:].indirect(l3[:]))
@@ -124,8 +130,6 @@ def tile_picked_codegain_store_bank_boardpair_one_plain_kernel(
         xo_bytes = sbuf("xo_bytes", [P, J], U8)
         nc.vector.tensor_copy(out=xo_bytes[:], in_=xo_plane[:].indirect(l4[:]))
 
-        w2_plane = sbuf("w2_plane", [P, R], U8)
-        spread_scale_rows(w2_plane, w2_stage, 64, QUAD)
         w2_bytes = sbuf("w2_bytes", [P, PACK, P], U8)
         nc.vector.tensor_copy(out=w2_bytes[:], in_=w2_plane[:].rearrange("p (m t) -> p t m", t=PACK))
 
@@ -148,7 +152,7 @@ def tile_picked_codegain_store_bank_boardpair_one_plain_kernel(
             out=w2_codes[:].bitcast(U16).rearrange("p (t m) -> p t m", t=PACK),
             in_=w2_sb[:].bitcast(U16).rearrange("p (m t) -> p t m", t=PACK),
         )
-        xc_codes = sbuf("xc_codes", [P, J], U32)
+        xc_codes = sbuf("xc_codes", [P, J], U32, tag="xo_sb")
         xc_bytes = sbuf("xc_bytes", [P, J], U8)
         nc.vector.quantize_mx(out=xc_codes[:].bitcast(FP8X4), scales=xc_bytes[:], in_=xc_bf[:].rearrange("p j t -> p (j t)"))
 
@@ -166,11 +170,11 @@ def tile_picked_codegain_store_bank_boardpair_one_plain_kernel(
                 rhs=xo_codes[:].bitcast(FP8X4), rhs_scale=xo_bytes[:], start=opens, stop=not opens,
             )
 
-        store_pass(0, True)
-        notes_pass(0, False)
+        notes_pass(0, True)
+        store_pass(0, False)
         for t in range(1, PACK):
-            notes_pass(t, True)
-            store_pass(t, False)
+            store_pass(t, True)
+            notes_pass(t, False)
 
         first = sbuf("first", [P, PACK, O], F32)
         second = sbuf("second", [P, PACK, O], F32)

from contextlib import ExitStack

import concourse.mybir as mybir

FLOPS = 301989888

F32 = mybir.dt.float32
BF16 = mybir.dt.bfloat16
I32 = mybir.dt.int32
U32 = mybir.dt.uint32
U16 = mybir.dt.uint16
U8 = mybir.dt.uint8
FP8X4 = mybir.dt.float8_e4m3fn_x4
FP4X4 = mybir.dt.float4_e2m1fn_x4
ACT = mybir.ActivationFunctionType
ALU = mybir.AluOpType

P = 128
PACK = 4
QUAD = 32
J, R, T, M, O, C, N = 256, 512, 1024, 1024, 128, 512, 256
WT_ROW = 4


def tile_picked_codegain_store_bank_boardpair_one_plain_kernel(
    tc, ta, tb, ga, gb, wt_words, wt_scales, xo_words, xo_scales, w2_words, w2_scales, sa, sb,
    wb_words, wb_scales, offs, offs2, offs3, offs4, offs5, offs6, offs7, out,
):
    nc = tc.nc
    with ExitStack() as ctx:
        lists = ctx.enter_context(tc.tile_pool(name="lists", bufs=1))
        keep = ctx.enter_context(tc.tile_pool(name="keep", bufs=1))
        psum = ctx.enter_context(tc.psum_pool(name="psum", bufs=1))

        def sbuf(name, shape, dtype, tag=None):
            return keep.tile(shape, dtype, name=name, tag=tag or name, align_bytes=64)

        def load_list(name, src):
            tile = lists.tile(list(src.shape), U16, name=name)
            nc.sync.dma_start(tile[:], src)
            return tile

        def load_column(name, src, queue):
            tile = sbuf(name, [P, PACK], F32)
            queue.dma_start(out=tile[:], in_=src.rearrange("(p t) o -> p (t o)", t=PACK))
            return tile

        def load_rows(name, src, t):
            tile = sbuf(name, [P, T], F32)
            nc.sync.dma_start(out=tile[:], in_=src.rearrange("(p t) c -> p t c", t=PACK)[:, t, :])
            return tile

        def load_scale_rows(stage, first, src):
            nc.gpsimd.dma_start(
                out=stage[first:first + 4, :, :].bitcast(I32),
                in_=src[0].rearrange("(q i) n -> i q n", i=4).bitcast(I32),
            )

        def load_plane_rows(plane, src, q):
            nc.sync.dma_start(
                out=plane[QUAD * q:QUAD * q + 4, :].bitcast(I32),
                in_=src[0, 4 * q:4 * q + 4, :].bitcast(I32),
            )

        def spread_scale_rows(plane, stage, first, rows):
            for q in range(4):
                nc.vector.tensor_copy(
                    out=plane[QUAD * q:QUAD * q + rows, :].bitcast(I32),
                    in_=stage[first:first + rows, q, :].bitcast(I32),
                )

        wt_stage = sbuf("wt_stage", [QUAD, 4, T], U8)
        nc.vector.memset(wt_stage[:].rearrange("p q n -> p (q n)").bitcast(I32), 0)
        w2_plane = sbuf("w2_plane", [P, R], U8)
        nc.vector.memset(w2_plane[:].bitcast(I32), 0)
        xo_plane = sbuf("xo_plane", [P, M], U8)
        nc.vector.memset(xo_plane[:].bitcast(I32), 0)
        wb_plane = sbuf("wb_plane", [P, N], U8)
        nc.vector.memset(wb_plane[:].bitcast(I32), 0)

        xo_stage = sbuf("xo_stage", [4, 4, M], U8)
        load_scale_rows(xo_stage, 0, xo_scales)
        load_scale_rows(wt_stage, WT_ROW, wt_scales)
        board = [sbuf("board%d" % t, [P, C], F32) for t in range(PACK)]
        for t in range(PACK):
            nc.gpsimd.memset(board[t][:], 0.0)
        ga_sb = load_column("ga_sb", ga, nc.scalar)
        gb_sb = load_column("gb_sb", gb, nc.scalar)
        wt_sb = sbuf("wt_sb", [P, T], U32)
        nc.sync.dma_start(out=wt_sb[:].bitcast(I32), in_=wt_words[0].rearrange("p n t -> p (n t)").bitcast(I32))
        l3 = load_list("l3", offs3)
        l1 = load_list("l1", offs)
        ta_sb, tb_sb = [], []
        ta_sb.append(load_rows("ta0", ta, 0))
        l2 = load_list("l2", offs2)
        tb_sb.append(load_rows("tb0", tb, 0))
        l4 = load_list("l4", offs4)
        ta_sb.append(load_rows("ta1", ta, 1))
        load_plane_rows(w2_plane, w2_scales, 0)
        tb_sb.append(load_rows("tb1", tb, 1))
        load_plane_rows(w2_plane, w2_scales, 1)
        ta_sb.append(load_rows("ta2", ta, 2))
        load_plane_rows(w2_plane, w2_scales, 2)
        tb_sb.append(load_rows("tb2", tb, 2))
        load_plane_rows(w2_plane, w2_scales, 3)
        ta_sb.append(load_rows("ta3", ta, 3))
        sa_sb = load_column("sa_sb", sa, nc.sync)
        tb_sb.append(load_rows("tb3", tb, 3))
        sb_sb = load_column("sb_sb", sb, nc.sync)
        w2_sb = sbuf("w2_sb", [P, 2 * R], U8)
        nc.sync.dma_start(out=w2_sb[:].bitcast(I32), in_=w2_words[0].bitcast(I32))
        xo_sb = sbuf("xo_sb", [P, M], U32)
        nc.sync.dma_start(out=xo_sb[:].bitcast(I32), in_=xo_words[0].rearrange("p n t -> p (n t)").bitcast(I32))
        l5 = load_list("l5", offs5)
        l6 = load_list("l6", offs6)
        l7 = load_list("l7", offs7)
        wb_sb = sbuf("wb_sb", [P, 2 * N], U8)
        nc.sync.dma_start(out=wb_sb[:].bitcast(I32), in_=wb_words[0].bitcast(I32))
        for q in range(4):
            load_plane_rows(wb_plane, wb_scales, q)

        wt_codes = sbuf("wt_codes", [P, PACK, P], U32)
        nc.vector.tensor_copy(out=wt_codes[:].rearrange("p t m -> p m t"), in_=wt_sb[:].indirect(l3[:]))
        wt_plane = sbuf("wt_plane", [P, T], U8)
        spread_scale_rows(wt_plane, wt_stage, 0, QUAD)
        wt_bytes = sbuf("wt_bytes", [P, PACK, P], U8)
        nc.vector.tensor_copy(out=wt_bytes[:].rearrange("p t m -> p m t"), in_=wt_plane[:].indirect(l3[:]))

        spread_scale_rows(xo_plane, xo_stage, 0, 4)
        xo_bytes = sbuf("xo_bytes", [P, J], U8)
        nc.vector.tensor_copy(out=xo_bytes[:], in_=xo_plane[:].indirect(l4[:]))

        w2_bytes = sbuf("w2_bytes", [P, PACK, P], U8)
        nc.vector.tensor_copy(out=w2_bytes[:], in_=w2_plane[:].rearrange("p (m t) -> p t m", t=PACK))

        xa = sbuf("xa", [P, PACK, J], F32)
        xb = sbuf("xb", [P, PACK, J], F32)
        xc_bf = sbuf("xc_bf", [P, J, PACK], BF16)
        for t in range(PACK):
            nc.scalar.activation(out=xa[:, t, :], in_=ta_sb[t][:].indirect(l1[:]), func=ACT.Copy, scale=ga_sb[:, t:t + 1])
            nc.scalar.activation(out=xb[:, t, :], in_=tb_sb[t][:].indirect(l2[:]), func=ACT.Copy, scale=gb_sb[:, t:t + 1])
            if t % 2 == 1:
                pair = slice(t - 1, t + 1)
                nc.vector.tensor_tensor(
                    out=xc_bf[:, :, pair], in0=xa[:, pair, :].rearrange("p t j -> p j t"),
                    in1=xb[:, pair, :].rearrange("p t j -> p j t"), op=ALU.mult,
                )
        xo_codes = sbuf("xo_codes", [P, J], U32)
        nc.vector.tensor_copy(out=xo_codes[:], in_=xo_sb[:].indirect(l4[:]))
        w2_codes = sbuf("w2_codes", [P, 2 * R], U8)
        nc.scalar.copy(
            out=w2_codes[:].bitcast(U16).rearrange("p (t m) -> p t m", t=PACK),
            in_=w2_sb[:].bitcast(U16).rearrange("p (m t) -> p t m", t=PACK),
        )
        xc_codes = sbuf("xc_codes", [P, J], U32, tag="xo_sb")
        xc_bytes = sbuf("xc_bytes", [P, J], U8)
        nc.vector.quantize_mx(out=xc_codes[:].bitcast(FP8X4), scales=xc_bytes[:], in_=xc_bf[:].rearrange("p j t -> p (j t)"))

        acc = [psum.tile([P, J], F32, name="acc%d" % t) for t in range(PACK)]

        def store_pass(t, opens):
            nc.tensor.matmul_mx(
                out=acc[t][:], lhsT=wt_codes[:, t, :].bitcast(FP8X4), lhsT_scale=wt_bytes[WT_ROW:P, t, :],
                rhs=xc_codes[:].bitcast(FP8X4), rhs_scale=xc_bytes[:], start=opens, stop=not opens,
            )

        def notes_pass(t, opens):
            nc.tensor.matmul_mx(
                out=acc[t][:], lhsT=w2_codes[:, 2 * P * t:2 * P * (t + 1)].bitcast(FP4X4), lhsT_scale=w2_bytes[:, t, :],
                rhs=xo_codes[:].bitcast(FP8X4), rhs_scale=xo_bytes[:], start=opens, stop=not opens,
            )

        notes_pass(0, True)
        store_pass(0, False)
        for t in range(1, PACK):
            store_pass(t, True)
            notes_pass(t, False)

        first = sbuf("first", [P, PACK, O], F32)
        second = sbuf("second", [P, PACK, O], F32)
        hidden = [sbuf("hidden%d" % t, [P, J], F32) for t in range(PACK)]
        for t in range(PACK):
            nc.scalar.copy(out=hidden[t][:], in_=acc[t][:])
        for t in range(PACK):
            nc.vector.tensor_copy(out=board[t][:].indirect(l5[:]), in_=hidden[t][:])
            nc.scalar.activation(out=first[:, t, :], in_=board[t][:].indirect(l6[:]), func=ACT.Copy, scale=sa_sb[:, t:t + 1])
            nc.scalar.activation(out=second[:, t, :], in_=board[t][:].indirect(l7[:]), func=ACT.Copy, scale=sb_sb[:, t:t + 1])

        diff = sbuf("diff", [P, PACK, O], F32)
        nc.vector.tensor_tensor(out=diff[:, 0:3, :], in0=first[:, 0:3, :], in1=second[:, 0:3, :], op=ALU.subtract)
        nc.vector.tensor_tensor(out=diff[:, 3, :], in0=first[:, 3, :], in1=second[:, 3, :], op=ALU.subtract)
        hid_bf = sbuf("hid_bf", [P, O, PACK], BF16)
        turned = diff[:].rearrange("p t o -> p o t")
        half = O // 2
        nc.scalar.activation(out=hid_bf[:, 0:half, :], in_=turned[:, 0:half, :], func=ACT.Abs)
        nc.vector.scalar_tensor_tensor(
            out=hid_bf[:, half:O, :], in0=turned[:, half:O, :], scalar=-1.0, in1=turned[:, half:O, :],
            op0=ALU.mult, op1=ALU.max,
        )
        hid_codes = sbuf("hid_codes", [P, O], U32)
        hid_bytes = sbuf("hid_bytes", [P, O], U8)
        nc.vector.quantize_mx(out=hid_codes[:].bitcast(FP8X4), scales=hid_bytes[:], in_=hid_bf[:].rearrange("p o t -> p (o t)"))

        for s, (copy, queue) in enumerate(((nc.scalar.copy, nc.scalar), (nc.vector.tensor_copy, nc.sync))):
            final = psum.tile([P, O], F32, name="final%d" % s)
            nc.tensor.matmul_mx(
                out=final[:], lhsT=wb_sb[:, 2 * P * s:2 * P * (s + 1)].bitcast(FP4X4), lhsT_scale=wb_plane[:, P * s:P * (s + 1)],
                rhs=hid_codes[:].bitcast(FP8X4), rhs_scale=hid_bytes[:], start=True, stop=True,
            )
            result = sbuf("result%d" % s, [P, O], F32)
            copy(out=result[:], in_=final[:])
            queue.dma_start(out=out[P * s:P * (s + 1), :], in_=result[:])
